import numpy as np
import ml_dtypes


def mxq(x, axis, fmt="e4m3"):
    dtype, down = {"e4m3": (ml_dtypes.float8_e4m3fn, 7), "e5m2": (ml_dtypes.float8_e5m2, 14)}[fmt]
    v = np.moveaxis(np.asarray(x, np.float32).astype(ml_dtypes.bfloat16).astype(np.float64), axis, -1)
    blocks = v.reshape(v.shape[:-1] + (-1, 32))
    amax = np.abs(blocks).max(-1, keepdims=True)
    byte = np.maximum(np.where(amax > 0, np.frexp(amax)[1] - 1 + 127, 0) - down, 1)
    scale = np.exp2(byte - 127.0)
    codes = (blocks / scale).astype(np.float32).astype(dtype).astype(np.float64)
    return np.moveaxis((codes * scale).reshape(v.shape), -1, axis)


WIDE = False


def mx_kscale(k):
    if not WIDE:
        return np.ones(k)
    levels = np.array([10, -10, 5, -5, 0])
    if k % 512:
        return np.exp2(np.random.permutation(np.resize(levels, k // 32))).repeat(32)
    a = np.empty((k // 512, 16))
    for p in range(k // 512):
        a[p, :8] = np.random.permutation(np.resize(levels, 8))
        for g in range(8):
            far = levels[np.abs(levels - a[p, g]) >= 10]
            a[p, g + 8] = far[np.random.randint(len(far))]
    return np.exp2(a.ravel()).repeat(32)


def f64(x):
    return np.asarray(x).astype(np.float64)


def striped8(idx):
    return np.asarray(idx).reshape(8, -1, 16).transpose(0, 2, 1).reshape(128, -1).astype(np.uint16)


def unstriped8(offs):
    return offs.reshape(8, 16, -1).transpose(0, 2, 1).reshape(8, -1).astype(np.int64)


def pick8(x, idx, run):
    r = np.arange(len(x))
    return x[r[:, None], idx[r % (8 * run) // run]]


E2M1 = np.array([0.0, 0.5, 1.0, 1.5, 2.0, 3.0, 4.0, 6.0, -0.0, -0.5, -1.0, -1.5, -2.0, -3.0, -4.0, -6.0])


def pack_weight(w, fmt):
    k, n = w.shape
    w = f64(np.asarray(w, np.float32).astype(ml_dtypes.bfloat16)).reshape(k // 32, 32, n)
    amax = np.abs(w).max(1)
    if fmt == "e4m3":
        byte = np.frexp(amax)[1] - 1 + 127 - 7
    else:
        mant, ex = np.frexp(amax / 6.0)
        byte = np.where(mant > 0.5, ex, ex - 1) + 127
    byte = np.clip(np.where(amax > 0, byte, 1), 1, 254)
    scaled = (w * np.exp2(127.0 - byte)[:, None, :]).reshape(k, n).astype(np.float32)
    by_word = np.ascontiguousarray(scaled.reshape(k // 512, 128, 4, n).transpose(0, 1, 3, 2))
    if fmt == "e4m3":
        words = by_word.astype(ml_dtypes.float8_e4m3fn).view(np.uint8)
    else:
        c = by_word.astype(ml_dtypes.float4_e2m1fn).view(np.uint8) & 0xF
        words = (c[..., 0::2] | (c[..., 1::2] << 4)).reshape(k // 512, 128, 2 * n)
    return np.ascontiguousarray(words), np.ascontiguousarray(byte.astype(np.uint8).reshape(k // 512, 16, n))


def unpack_weight(words, scales, fmt):
    g, _, n = scales.shape
    words = np.ascontiguousarray(words).reshape(g, 128, n, -1)
    if fmt == "e4m3":
        vals = words.view(ml_dtypes.float8_e4m3fn).astype(np.float64)
    else:
        nib = np.empty((g, 128, n, 4), np.uint8)
        nib[..., 0::2] = words & 0xF
        nib[..., 1::2] = words >> 4
        vals = E2M1[nib]
    vals = vals * np.repeat(np.exp2(scales.astype(np.float64) - 127.0), 8, axis=1)[..., None]
    return vals.transpose(0, 1, 3, 2).reshape(g * 512, n)


D, T, I, Q = 512, 1024, 512, 128


def setup_inputs():
    n = np.random.standard_normal
    idx = np.stack([np.random.permutation(T)[:I] for _ in range(8)])
    idx2 = np.stack([np.random.permutation(T)[:I] for _ in range(8)])
    idx3 = np.stack([np.random.permutation(T)[:I] for _ in range(8)])
    idx4 = np.stack([np.random.permutation(T)[:I] for _ in range(8)])
    fd = mx_kscale(D)
    keysp = pack_weight(n((D, T)) / fd[:, None], "e2m1")
    return {
        "query": (n((D, Q)) * 1.2 / np.sqrt(D) * fd[:, None]).astype(np.float32),
        "keys_words": keysp[0],
        "keys_scales": keysp[1],
        "lam": (np.random.uniform(0.8, 1.8, (Q, 1))).astype(np.float32),
        "old": (1.0 * n((Q, T))).astype(np.float32),
        "share2": (np.random.uniform(0.4, 1.2, (Q, 1))).astype(np.float32),
        "offs": striped8(idx),
        "offs2": striped8(idx2),
        "offs3": striped8(idx3),
        "offs4": striped8(idx4),
    }


def reference(query, keys_words, keys_scales, lam, old, share2, offs, offs2, offs3, offs4):
    idx = unstriped8(offs)
    idx2 = unstriped8(offs2)
    idx3 = unstriped8(offs3)
    idx4 = unstriped8(offs4)
    keysu = unpack_weight(keys_words, keys_scales, "e2m1")
    queryq = mxq(f64(query), 0, "e4m3")
    a = queryq.T @ keysu
    lo2 = np.minimum(pick8(a, idx, 16), pick8(a, idx2, 16))
    hi2 = np.maximum(pick8(a, idx, 16), pick8(a, idx2, 16))
    s = np.maximum(lo2, np.minimum(hi2, pick8(a, idx3, 16))) * f64(lam)
    w = np.maximum(s, 0.0)
    f1 = np.zeros((Q, T))
    f1[np.arange(Q)[:, None], idx[np.arange(Q) % 128 // 16]] = w
    f2 = np.zeros((Q, T))
    f2[np.arange(Q)[:, None], idx4[np.arange(Q) % 128 // 16]] = w
    y = f64(old) + f1 + f2 * f64(share2)
    return y

@@ -1,0 +1,177 @@
+from contextlib import ExitStack
+
+import concourse.mybir as mybir
+
+D, T, I, Q = 512, 1024, 512, 128
+FLOPS = 2 * D * T * Q
+
+F32 = mybir.dt.float32
+BF16 = mybir.dt.bfloat16
+I32 = mybir.dt.int32
+U32 = mybir.dt.uint32
+U16 = mybir.dt.uint16
+U8 = mybir.dt.uint8
+FP8X4 = mybir.dt.float8_e4m3fn_x4
+FP4X4 = mybir.dt.float4_e2m1fn_x4
+ALU = mybir.AluOpType
+ACT = mybir.ActivationFunctionType
+
+P = 128
+PACK = 4
+LANES = 16
+MM_WIDTHS = (256, 256, 256, 128, 128)
+BIG = 3.0e38
+HALF = I // 2
+QUARTER = I // 4
+N_OUT = 256
+
+
+def tile_attend_middle_lean_twiceput_heads_kernel(
+    tc, query, keys_words, keys_scales, lam, old, share2, offs, offs2, offs3, offs4, out
+):
+    nc = tc.nc
+    with ExitStack() as ctx:
+        lists = ctx.enter_context(tc.tile_pool(name="lists", bufs=1))
+        sb = ctx.enter_context(tc.tile_pool(name="sb", bufs=1))
+        ps = ctx.enter_context(tc.psum_pool(name="ps", bufs=1))
+
+        q_raw = sb.tile([P, PACK, Q], F32, name="q_raw")
+        nc.sync.dma_start(out=q_raw[:], in_=query.rearrange("(p j) q -> p j q", j=PACK))
+
+        k_scales = sb.tile([P, T], U8, name="k_scales", align_bytes=64)
+        for quad in range(4):
+            nc.scalar.dma_start(
+                out=k_scales[32 * quad : 32 * quad + 4, :].bitcast(I32),
+                in_=keys_scales[0, 4 * quad : 4 * quad + 4, :].bitcast(I32),
+            )
+        k_words = sb.tile([P, 2 * T], U8, name="k_words", align_bytes=64)
+        nc.sync.dma_start(out=k_words[:].bitcast(I32), in_=keys_words[0].bitcast(I32))
+
+        def load_list(src, name):
+            tile = lists.tile([P, I // LANES], U16, name=name)
+            nc.sync.dma_start(tile[:], src)
+            return tile
+
+        idx1 = load_list(offs, "idx1")
+        idx2 = load_list(offs2, "idx2")
+        idx3 = load_list(offs3, "idx3")
+        lam_sb = sb.tile([P, 1], F32, name="lam_sb")
+        nc.sync.dma_start(out=lam_sb[:], in_=lam)
+        idx4 = load_list(offs4, "idx4")
+        old_sb = sb.tile([P, T], F32, name="old_sb")
+        nc.sync.dma_start(out=old_sb[:], in_=old)
+        share_sb = sb.tile([P, 1], F32, name="share_sb")
+        nc.sync.dma_start(out=share_sb[:], in_=share2)
+
+        f1 = sb.tile([P, T], F32, name="f1")
+        f2 = sb.tile([P, T], F32, name="f2")
+        nc.vector.memset(f1[:], 0.0)
+        nc.vector.memset(f2[:], 0.0)
+
+        q_bf = sb.tile([P, Q, PACK], BF16, name="q_bf", align_bytes=64)
+        nc.vector.tensor_copy(
+            out=q_bf[:].rearrange("p (c i) j -> p c j i", i=4),
+            in_=q_raw[:].rearrange("p j (c i) -> p c j i", i=4),
+        )
+        q_codes = sb.tile([P, Q], U32, name="q_codes", align_bytes=64)
+        q_scales = sb.tile([P, Q], U8, name="q_scales", align_bytes=64)
+        nc.vector.quantize_mx(
+            out=q_codes[:].bitcast(FP8X4), scales=q_scales[:], in_=q_bf[:].rearrange("p q j -> p (q j)")
+        )
+
+        a = sb.tile([P, T], F32, name="a")
+        first = 0
+        for n, width in enumerate(MM_WIDTHS):
+            cols = slice(first, first + width)
+            bank = ps.tile([P, width], F32, name=f"bank{n}")
+            nc.tensor.matmul_mx(
+                out=bank[:],
+                lhsT=q_codes[:].bitcast(FP8X4),
+                lhsT_scale=q_scales[:],
+                rhs=k_words[:, 2 * first : 2 * (first + width)].bitcast(FP4X4),
+                rhs_scale=k_scales[:, cols],
+                start=True,
+                stop=True,
+            )
+            if n % 2 == 1:
+                nc.scalar.copy(out=a[:, cols], in_=bank[:])
+            else:
+                nc.vector.tensor_copy(out=a[:, cols], in_=bank[:])
+            first = first + width
+
+        def entries(idx, first, count):
+            return idx[:, first // LANES : (first + count) // LANES]
+
+        def half_tile(name, h):
+            return sb.tile([P, HALF], F32, name=f"{name}{h}")
+
+        x = [half_tile("x", h) for h in range(2)]
+        y = [half_tile("y", h) for h in range(2)]
+        z = [half_tile("z", h) for h in range(2)]
+        work = [half_tile("work", n) for n in range(3)]
+        hi = [work[0], work[1]]
+        lo = [work[1], work[2]]
+        mid = [work[2], work[0]]
+        med = [half_tile("med", h) for h in range(2)]
+        w = sb.tile([P, I], F32, name="w")
+
+        def gather_scalar(dst, idx, h):
+            nc.scalar.activation(dst[h][:], a[:].indirect(entries(idx, h * HALF, HALF)), ACT.Copy)
+
+        def gather_vector(dst, idx, h):
+            nc.vector.tensor_copy(dst[h][:], a[:].indirect(entries(idx, h * HALF, HALF)))
+
+        top = sb.tile([P, 1], F32, name="top")
+        bottom = sb.tile([P, 1], F32, name="bottom")
+        nc.gpsimd.tensor_scalar(top[:], lam_sb[:], 0.0, BIG, ALU.is_ge, ALU.mult)
+        nc.gpsimd.tensor_scalar(bottom[:], lam_sb[:], 0.0, -BIG, ALU.is_lt, ALU.mult)
+        lam_wide = sb.tile([P, HALF], F32, name="lam_wide")
+        nc.scalar.copy(out=lam_wide[:], in_=lam_sb[:].to_broadcast([P, HALF]))
+
+        def bounds(h):
+            nc.vector.tensor_tensor(hi[h][:], x[h][:], y[h][:], ALU.max)
+            nc.vector.scalar_tensor_tensor(lo[h][:], x[h][:], top[:], y[h][:], ALU.min, ALU.min)
+            nc.vector.scalar_tensor_tensor(mid[h][:], hi[h][:], top[:], z[h][:], ALU.min, ALU.min)
+
+        def median(h):
+            nc.vector.scalar_tensor_tensor(med[h][:], lo[h][:], bottom[:], mid[h][:], ALU.max, ALU.max)
+
+        def weight_scalar(h):
+            nc.scalar.activation(w[:, h * HALF : (h + 1) * HALF], med[h][:], ACT.Copy, scale=lam_sb[:])
+
+        def put_first(h, first, count):
+            nc.vector.tensor_tensor(
+                f1[:].indirect(entries(idx1, h * HALF + first, count)),
+                med[h][:, first : first + count],
+                lam_wide[:, 0:count],
+                ALU.mult,
+            )
+
+        def put(dst, idx, first, count):
+            nc.vector.tensor_copy(dst[:].indirect(entries(idx, first, count)), w[:, first : first + count])
+
+        gather_vector(x, idx1, 0)
+        gather_scalar(y, idx2, 0)
+        gather_scalar(z, idx3, 0)
+        gather_scalar(x, idx1, 1)
+        gather_scalar(y, idx2, 1)
+        gather_scalar(z, idx3, 1)
+        bounds(0)
+        median(0)
+        put_first(0, 0, QUARTER)
+        bounds(1)
+        put_first(0, QUARTER, QUARTER)
+        median(1)
+        weight_scalar(0)
+        weight_scalar(1)
+        put_first(1, 0, HALF)
+        put(f2, idx4, 0, I)
+        part = sb.tile([P, T], F32, name="part")
+        nc.gpsimd.tensor_tensor(part[:], old_sb[:], f1[:], ALU.add)
+
+        res = sb.tile([P, T], F32, name="res")
+        for n in range(T // N_OUT):
+            cols = slice(n * N_OUT, (n + 1) * N_OUT)
+            nc.vector.scalar_tensor_tensor(res[:, cols], f2[:, cols], share_sb[:], part[:, cols], ALU.mult, ALU.add)
+            queue = nc.sync if n % 2 == 0 else nc.scalar
+            queue.dma_start(out=out[:, cols], in_=res[:, cols])

@@ -1,6 +1,7 @@
 from contextlib import ExitStack
 
 import concourse.mybir as mybir
+from concourse.masks import make_identity
 
 D, T, I, Q = 512, 1024, 512, 128
 FLOPS = 2 * D * T * Q
@@ -19,11 +20,14 @@ ACT = mybir.ActivationFunctionType
 P = 128
 PACK = 4
 LANES = 16
+BANKS = 8
 MM_WIDTHS = (256, 256, 256, 128, 128)
 BIG = 3.0e38
 HALF = I // 2
 QUARTER = I // 4
-N_OUT = 256
+CHUNK = 384
+CHUNKS = 1
+OUT_WIDTHS = (128, 256, 256, 256, 128)
 
 
 def tile_attend_middle_lean_twiceput_heads_kernel(
@@ -35,55 +39,70 @@ def tile_attend_middle_lean_twiceput_heads_kernel(
         sb = ctx.enter_context(tc.tile_pool(name="sb", bufs=1))
         ps = ctx.enter_context(tc.psum_pool(name="ps", bufs=1))
 
-        q_raw = sb.tile([P, PACK, Q], F32, name="q_raw")
-        nc.sync.dma_start(out=q_raw[:], in_=query.rearrange("(p j) q -> p j q", j=PACK))
-
-        k_scales = sb.tile([P, T], U8, name="k_scales", align_bytes=64)
-        for quad in range(4):
-            nc.scalar.dma_start(
-                out=k_scales[32 * quad : 32 * quad + 4, :].bitcast(I32),
-                in_=keys_scales[0, 4 * quad : 4 * quad + 4, :].bitcast(I32),
-            )
-        k_words = sb.tile([P, 2 * T], U8, name="k_words", align_bytes=64)
-        nc.sync.dma_start(out=k_words[:].bitcast(I32), in_=keys_words[0].bitcast(I32))
+        def bank_tile(n, width):
+            return ps.tile([P, width], F32, name=f"bank{n % BANKS}")
 
         def load_list(src, name):
             tile = lists.tile([P, I // LANES], U16, name=name)
             nc.sync.dma_start(tile[:], src)
             return tile
 
+        q_raw = [sb.tile([P, 2, Q], F32, name=f"q_raw{u}") for u in range(2)]
+        k_scales = sb.tile([P, T], U8, name="k_scales", align_bytes=64)
+        k_words = sb.tile([P, 2 * T], U8, name="k_words", align_bytes=64)
+        lam_sb = sb.tile([P, 1], F32, name="lam_sb")
+        old_sb = sb.tile([P, T], F32, name="old_sb")
+        share_sb = sb.tile([P, 1], F32, name="share_sb")
+
+        def load_scales(queue, quad):
+            queue.dma_start(
+                out=k_scales[32 * quad : 32 * quad + 4, :].bitcast(I32),
+                in_=keys_scales[0, 4 * quad : 4 * quad + 4, :].bitcast(I32),
+            )
+
+        q_rows = query.rearrange("(p j) q -> p j q", j=PACK)
+        for u in range(2):
+            nc.sync.dma_start(out=q_raw[u][:], in_=q_rows[:, 2 * u : 2 * u + 2, :])
+        for quad in range(4):
+            load_scales(nc.scalar, quad)
+        nc.sync.dma_start(out=k_words[:].bitcast(I32), in_=keys_words[0].bitcast(I32))
+        nc.sync.dma_start(out=lam_sb[:], in_=lam)
         idx1 = load_list(offs, "idx1")
         idx2 = load_list(offs2, "idx2")
         idx3 = load_list(offs3, "idx3")
-        lam_sb = sb.tile([P, 1], F32, name="lam_sb")
-        nc.sync.dma_start(out=lam_sb[:], in_=lam)
-        idx4 = load_list(offs4, "idx4")
-        old_sb = sb.tile([P, T], F32, name="old_sb")
         nc.sync.dma_start(out=old_sb[:], in_=old)
-        share_sb = sb.tile([P, 1], F32, name="share_sb")
+        idx4 = load_list(offs4, "idx4")
         nc.sync.dma_start(out=share_sb[:], in_=share2)
 
         f1 = sb.tile([P, T], F32, name="f1")
         f2 = sb.tile([P, T], F32, name="f2")
         nc.vector.memset(f1[:], 0.0)
         nc.vector.memset(f2[:], 0.0)
+        ident = sb.tile([P, P], F32, name="ident")
+        make_identity(nc, ident[:])
 
-        q_bf = sb.tile([P, Q, PACK], BF16, name="q_bf", align_bytes=64)
-        nc.vector.tensor_copy(
-            out=q_bf[:].rearrange("p (c i) j -> p c j i", i=4),
-            in_=q_raw[:].rearrange("p j (c i) -> p c j i", i=4),
-        )
+        q_bf = sb.tile([P, Q, PACK], BF16, name="q_bf", tag="q_bf_then_lam", align_bytes=64)
+        for u in range(2):
+            nc.vector.tensor_copy(out=q_bf[:, :, 2 * u : 2 * u + 2], in_=q_raw[u][:].rearrange("p j q -> p q j"))
         q_codes = sb.tile([P, Q], U32, name="q_codes", align_bytes=64)
         q_scales = sb.tile([P, Q], U8, name="q_scales", align_bytes=64)
         nc.vector.quantize_mx(
             out=q_codes[:].bitcast(FP8X4), scales=q_scales[:], in_=q_bf[:].rearrange("p q j -> p (q j)")
         )
 
+        from_lam = sb.tile([P, HALF + 2], F32, name="from_lam", tag="q_bf_then_lam", align_bytes=64)
+        lam_wide = from_lam[:, 0:HALF]
+        top = from_lam[:, HALF : HALF + 1]
+        bottom = from_lam[:, HALF + 1 : HALF + 2]
+        nc.vector.tensor_scalar(top, lam_sb[:], 0.0, BIG, ALU.is_ge, ALU.mult)
+        nc.vector.tensor_scalar(bottom, lam_sb[:], 0.0, -BIG, ALU.is_lt, ALU.mult)
+        nc.vector.tensor_copy(out=lam_wide, in_=lam_sb[:].to_broadcast([P, HALF]))
+
         a = sb.tile([P, T], F32, name="a")
         first = 0
         for n, width in enumerate(MM_WIDTHS):
             cols = slice(first, first + width)
-            bank = ps.tile([P, width], F32, name=f"bank{n}")
+            bank = bank_tile(n, width)
             nc.tensor.matmul_mx(
                 out=bank[:],
                 lhsT=q_codes[:].bitcast(FP8X4),
@@ -112,7 +131,7 @@ def tile_attend_middle_lean_twiceput_heads_kernel(
         hi = [work[0], work[1]]
         lo = [work[1], work[2]]
         mid = [work[2], work[0]]
-        med = [half_tile("med", h) for h in range(2)]
+        med = sb.tile([P, I], F32, name="med")
         w = sb.tile([P, I], F32, name="w")
 
         def gather_scalar(dst, idx, h):
@@ -121,34 +140,50 @@ def tile_attend_middle_lean_twiceput_heads_kernel(
         def gather_vector(dst, idx, h):
             nc.vector.tensor_copy(dst[h][:], a[:].indirect(entries(idx, h * HALF, HALF)))
 
-        top = sb.tile([P, 1], F32, name="top")
-        bottom = sb.tile([P, 1], F32, name="bottom")
-        nc.gpsimd.tensor_scalar(top[:], lam_sb[:], 0.0, BIG, ALU.is_ge, ALU.mult)
-        nc.gpsimd.tensor_scalar(bottom[:], lam_sb[:], 0.0, -BIG, ALU.is_lt, ALU.mult)
-        lam_wide = sb.tile([P, HALF], F32, name="lam_wide")
-        nc.scalar.copy(out=lam_wide[:], in_=lam_sb[:].to_broadcast([P, HALF]))
-
         def bounds(h):
             nc.vector.tensor_tensor(hi[h][:], x[h][:], y[h][:], ALU.max)
-            nc.vector.scalar_tensor_tensor(lo[h][:], x[h][:], top[:], y[h][:], ALU.min, ALU.min)
-            nc.vector.scalar_tensor_tensor(mid[h][:], hi[h][:], top[:], z[h][:], ALU.min, ALU.min)
+            nc.vector.scalar_tensor_tensor(lo[h][:], x[h][:], top, y[h][:], ALU.min, ALU.min)
 
-        def median(h):
-            nc.vector.scalar_tensor_tensor(med[h][:], lo[h][:], bottom[:], mid[h][:], ALU.max, ALU.max)
+        def third(h, first, count):
+            part = slice(first, first + count)
+            nc.vector.scalar_tensor_tensor(mid[h][:, part], hi[h][:, part], top, z[h][:, part], ALU.min, ALU.min)
+
+        def median(h, first, count):
+            part = slice(first, first + count)
+            dst = med[:, h * HALF + first : h * HALF + first + count]
+            nc.vector.scalar_tensor_tensor(dst, lo[h][:, part], bottom, mid[h][:, part], ALU.max, ALU.max)
 
         def weight_scalar(h):
-            nc.scalar.activation(w[:, h * HALF : (h + 1) * HALF], med[h][:], ACT.Copy, scale=lam_sb[:])
+            part = slice(h * HALF, (h + 1) * HALF)
+            nc.scalar.activation(w[:, part], med[:, part], ACT.Copy, scale=lam_sb[:])
 
-        def put_first(h, first, count):
+        def put_first(first, count):
             nc.vector.tensor_tensor(
-                f1[:].indirect(entries(idx1, h * HALF + first, count)),
-                med[h][:, first : first + count],
-                lam_wide[:, 0:count],
+                f1[:].indirect(entries(idx1, first, count)),
+                med[:, first : first + count],
+                from_lam[:, 0:count],
                 ALU.mult,
             )
 
-        def put(dst, idx, first, count):
-            nc.vector.tensor_copy(dst[:].indirect(entries(idx, first, count)), w[:, first : first + count])
+        def put_second(first, count):
+            nc.vector.tensor_copy(f2[:].indirect(entries(idx4, first, count)), w[:, first : first + count])
+
+        blocks = CHUNK // P
+        turned = [bank_tile(len(MM_WIDTHS) + c, CHUNK) for c in range(CHUNKS)]
+
+        def add_turned(src, c, opens):
+            for b in range(blocks):
+                nc.tensor.matmul(
+                    turned[c][:, b * P : (b + 1) * P],
+                    src[:, c * CHUNK + b * P : c * CHUNK + (b + 1) * P],
+                    ident[:],
+                    start=(opens and b == 0),
+                    stop=(not opens and b == blocks - 1),
+                    is_transpose=True,
+                )
+
+        for c in range(CHUNKS):
+            add_turned(old_sb, c, True)
 
         gather_vector(x, idx1, 0)
         gather_scalar(y, idx2, 0)
@@ -157,21 +192,46 @@ def tile_attend_middle_lean_twiceput_heads_kernel(
         gather_scalar(y, idx2, 1)
         gather_scalar(z, idx3, 1)
         bounds(0)
-        median(0)
-        put_first(0, 0, QUARTER)
+        third(0, 0, QUARTER)
+        third(0, QUARTER, QUARTER)
+        median(0, 0, QUARTER)
+        median(0, QUARTER, QUARTER)
+        put_first(0, QUARTER)
         bounds(1)
-        put_first(0, QUARTER, QUARTER)
-        median(1)
+        third(1, 0, HALF)
+        put_first(QUARTER, QUARTER)
+        median(1, 0, HALF)
         weight_scalar(0)
         weight_scalar(1)
-        put_first(1, 0, HALF)
-        put(f2, idx4, 0, I)
-        part = sb.tile([P, T], F32, name="part")
-        nc.gpsimd.tensor_tensor(part[:], old_sb[:], f1[:], ALU.add)
+        put_second(0, QUARTER)
+        put_first(HALF, HALF)
+        put_second(QUARTER, I - QUARTER)
+
+        for c in range(CHUNKS):
+            add_turned(f1, c, False)
+        base = []
+        for c in range(CHUNKS):
+            staged = sb.tile([P, CHUNK], F32, name=f"staged{c}")
+            nc.scalar.copy(out=staged[:], in_=turned[c][:])
+            back = bank_tile(len(MM_WIDTHS) + CHUNKS + c, CHUNK)
+            for b in range(blocks):
+                nc.tensor.transpose(back[:, b * P : (b + 1) * P], staged[:, b * P : (b + 1) * P], ident[:])
+            base.append(back)
+
+        turned_cols = CHUNKS * CHUNK
+        rest = sb.tile([P, T - turned_cols], F32, name="rest")
+        nc.gpsimd.tensor_tensor(rest[:], old_sb[:, turned_cols:T], f1[:, turned_cols:T], ALU.add)
 
         res = sb.tile([P, T], F32, name="res")
-        for n in range(T // N_OUT):
-            cols = slice(n * N_OUT, (n + 1) * N_OUT)
-            nc.vector.scalar_tensor_tensor(res[:, cols], f2[:, cols], share_sb[:], part[:, cols], ALU.mult, ALU.add)
+        first = 0
+        for n, width in enumerate(OUT_WIDTHS):
+            cols = slice(first, first + width)
+            if first < turned_cols:
+                start = first % CHUNK
+                addend = base[first // CHUNK][:, start : start + width]
+            else:
+                addend = rest[:, first - turned_cols : first - turned_cols + width]
+            nc.vector.scalar_tensor_tensor(res[:, cols], f2[:, cols], share_sb[:], addend, ALU.mult, ALU.add)
             queue = nc.sync if n % 2 == 0 else nc.scalar
             queue.dma_start(out=out[:, cols], in_=res[:, cols])
+            first = first + width

@@ -25,7 +25,7 @@ MM_WIDTHS = (256, 256, 256, 128, 128)
 BIG = 3.0e38
 HALF = I // 2
 QUARTER = I // 4
-CHUNK = 384
+CHUNK = 128
 CHUNKS = 1
 OUT_WIDTHS = (128, 256, 256, 256, 128)
 
@@ -47,7 +47,7 @@ def tile_attend_middle_lean_twiceput_heads_kernel(
             nc.sync.dma_start(tile[:], src)
             return tile
 
-        q_raw = [sb.tile([P, 2, Q], F32, name=f"q_raw{u}") for u in range(2)]
+        q_raw = sb.tile([P, PACK, Q], F32, name="q_raw")
         k_scales = sb.tile([P, T], U8, name="k_scales", align_bytes=64)
         k_words = sb.tile([P, 2 * T], U8, name="k_words", align_bytes=64)
         lam_sb = sb.tile([P, 1], F32, name="lam_sb")
@@ -60,9 +60,7 @@ def tile_attend_middle_lean_twiceput_heads_kernel(
                 in_=keys_scales[0, 4 * quad : 4 * quad + 4, :].bitcast(I32),
             )
 
-        q_rows = query.rearrange("(p j) q -> p j q", j=PACK)
-        for u in range(2):
-            nc.sync.dma_start(out=q_raw[u][:], in_=q_rows[:, 2 * u : 2 * u + 2, :])
+        nc.sync.dma_start(out=q_raw[:], in_=query.rearrange("(p j) q -> p j q", j=PACK))
         for quad in range(4):
             load_scales(nc.scalar, quad)
         nc.sync.dma_start(out=k_words[:].bitcast(I32), in_=keys_words[0].bitcast(I32))
@@ -82,8 +80,10 @@ def tile_attend_middle_lean_twiceput_heads_kernel(
         make_identity(nc, ident[:])
 
         q_bf = sb.tile([P, Q, PACK], BF16, name="q_bf", tag="q_bf_then_lam", align_bytes=64)
-        for u in range(2):
-            nc.vector.tensor_copy(out=q_bf[:, :, 2 * u : 2 * u + 2], in_=q_raw[u][:].rearrange("p j q -> p q j"))
+        nc.vector.tensor_copy(
+            out=q_bf[:].rearrange("p (c i) j -> p c j i", i=4),
+            in_=q_raw[:].rearrange("p j (c i) -> p c j i", i=4),
+        )
         q_codes = sb.tile([P, Q], U32, name="q_codes", align_bytes=64)
         q_scales = sb.tile([P, Q], U8, name="q_scales", align_bytes=64)
         nc.vector.quantize_mx(
@@ -175,7 +175,7 @@ def tile_attend_middle_lean_twiceput_heads_kernel(
             for b in range(blocks):
                 nc.tensor.matmul(
                     turned[c][:, b * P : (b + 1) * P],
-                    src[:, c * CHUNK + b * P : c * CHUNK + (b + 1) * P],
+                    src[:, T - CHUNK + b * P : T - CHUNK + (b + 1) * P],
                     ident[:],
                     start=(opens and b == 0),
                     stop=(not opens and b == blocks - 1),
@@ -218,19 +218,18 @@ def tile_attend_middle_lean_twiceput_heads_kernel(
                 nc.tensor.transpose(back[:, b * P : (b + 1) * P], staged[:, b * P : (b + 1) * P], ident[:])
             base.append(back)
 
-        turned_cols = CHUNKS * CHUNK
-        rest = sb.tile([P, T - turned_cols], F32, name="rest")
-        nc.gpsimd.tensor_tensor(rest[:], old_sb[:, turned_cols:T], f1[:, turned_cols:T], ALU.add)
+        plain_cols = T - CHUNK
+        rest = sb.tile([P, plain_cols], F32, name="rest")
+        nc.gpsimd.tensor_tensor(rest[:], old_sb[:, 0:plain_cols], f1[:, 0:plain_cols], ALU.add)
 
         res = sb.tile([P, T], F32, name="res")
         first = 0
         for n, width in enumerate(OUT_WIDTHS):
             cols = slice(first, first + width)
-            if first < turned_cols:
-                start = first % CHUNK
-                addend = base[first // CHUNK][:, start : start + width]
+            if first < plain_cols:
+                addend = rest[:, cols]
             else:
-                addend = rest[:, first - turned_cols : first - turned_cols + width]
+                addend = base[0][:, first - plain_cols : first - plain_cols + width]
             nc.vector.scalar_tensor_tensor(res[:, cols], f2[:, cols], share_sb[:], addend, ALU.mult, ALU.add)
             queue = nc.sync if n % 2 == 0 else nc.scalar
             queue.dma_start(out=out[:, cols], in_=res[:, cols])

from contextlib import ExitStack

import concourse.mybir as mybir
from concourse.masks import make_identity

D, T, I, Q = 512, 1024, 512, 128
FLOPS = 2 * D * T * Q

F32 = mybir.dt.float32
BF16 = mybir.dt.bfloat16
I32 = mybir.dt.int32
U32 = mybir.dt.uint32
U16 = mybir.dt.uint16
U8 = mybir.dt.uint8
FP8X4 = mybir.dt.float8_e4m3fn_x4
FP4X4 = mybir.dt.float4_e2m1fn_x4
ALU = mybir.AluOpType
ACT = mybir.ActivationFunctionType

P = 128
PACK = 4
LANES = 16
BANKS = 8
MM_WIDTHS = (256, 256, 256, 128, 128)
BIG = 3.0e38
HALF = I // 2
QUARTER = I // 4
CHUNK = 128
CHUNKS = 1
OUT_WIDTHS = (128, 256, 256, 256, 128)


def tile_attend_middle_lean_twiceput_heads_kernel(
    tc, query, keys_words, keys_scales, lam, old, share2, offs, offs2, offs3, offs4, out
):
    nc = tc.nc
    with ExitStack() as ctx:
        lists = ctx.enter_context(tc.tile_pool(name="lists", bufs=1))
        sb = ctx.enter_context(tc.tile_pool(name="sb", bufs=1))
        ps = ctx.enter_context(tc.psum_pool(name="ps", bufs=1))

        def bank_tile(n, width):
            return ps.tile([P, width], F32, name=f"bank{n % BANKS}")

        def load_list(src, name):
            tile = lists.tile([P, I // LANES], U16, name=name)
            nc.sync.dma_start(tile[:], src)
            return tile

        q_raw = sb.tile([P, PACK, Q], F32, name="q_raw")
        k_scales = sb.tile([P, T], U8, name="k_scales", align_bytes=64)
        k_words = sb.tile([P, 2 * T], U8, name="k_words", align_bytes=64)
        lam_sb = sb.tile([P, 1], F32, name="lam_sb")
        old_sb = sb.tile([P, T], F32, name="old_sb")
        share_sb = sb.tile([P, 1], F32, name="share_sb")

        def load_scales(queue, quad):
            queue.dma_start(
                out=k_scales[32 * quad : 32 * quad + 4, :].bitcast(I32),
                in_=keys_scales[0, 4 * quad : 4 * quad + 4, :].bitcast(I32),
            )

        nc.sync.dma_start(out=q_raw[:], in_=query.rearrange("(p j) q -> p j q", j=PACK))
        for quad in range(4):
            load_scales(nc.scalar, quad)
        nc.sync.dma_start(out=k_words[:].bitcast(I32), in_=keys_words[0].bitcast(I32))
        nc.sync.dma_start(out=lam_sb[:], in_=lam)
        idx1 = load_list(offs, "idx1")
        idx2 = load_list(offs2, "idx2")
        idx3 = load_list(offs3, "idx3")
        nc.sync.dma_start(out=old_sb[:], in_=old)
        idx4 = load_list(offs4, "idx4")
        nc.sync.dma_start(out=share_sb[:], in_=share2)

        f1 = sb.tile([P, T], F32, name="f1")
        f2 = sb.tile([P, T], F32, name="f2")
        nc.vector.memset(f1[:], 0.0)
        nc.vector.memset(f2[:], 0.0)
        ident = sb.tile([P, P], F32, name="ident")
        make_identity(nc, ident[:])

        q_bf = sb.tile([P, Q, PACK], BF16, name="q_bf", tag="q_bf_then_lam", align_bytes=64)
        nc.vector.tensor_copy(
            out=q_bf[:].rearrange("p (c i) j -> p c j i", i=4),
            in_=q_raw[:].rearrange("p j (c i) -> p c j i", i=4),
        )
        q_codes = sb.tile([P, Q], U32, name="q_codes", align_bytes=64)
        q_scales = sb.tile([P, Q], U8, name="q_scales", align_bytes=64)
        nc.vector.quantize_mx(
            out=q_codes[:].bitcast(FP8X4), scales=q_scales[:], in_=q_bf[:].rearrange("p q j -> p (q j)")
        )

        from_lam = sb.tile([P, HALF + 2], F32, name="from_lam", tag="q_bf_then_lam", align_bytes=64)
        lam_wide = from_lam[:, 0:HALF]
        top = from_lam[:, HALF : HALF + 1]
        bottom = from_lam[:, HALF + 1 : HALF + 2]
        nc.vector.tensor_scalar(top, lam_sb[:], 0.0, BIG, ALU.is_ge, ALU.mult)
        nc.vector.tensor_scalar(bottom, lam_sb[:], 0.0, -BIG, ALU.is_lt, ALU.mult)
        nc.vector.tensor_copy(out=lam_wide, in_=lam_sb[:].to_broadcast([P, HALF]))

        a = sb.tile([P, T], F32, name="a")
        first = 0
        for n, width in enumerate(MM_WIDTHS):
            cols = slice(first, first + width)
            bank = bank_tile(n, width)
            nc.tensor.matmul_mx(
                out=bank[:],
                lhsT=q_codes[:].bitcast(FP8X4),
                lhsT_scale=q_scales[:],
                rhs=k_words[:, 2 * first : 2 * (first + width)].bitcast(FP4X4),
                rhs_scale=k_scales[:, cols],
                start=True,
                stop=True,
            )
            if n % 2 == 1:
                nc.scalar.copy(out=a[:, cols], in_=bank[:])
            else:
                nc.vector.tensor_copy(out=a[:, cols], in_=bank[:])
            first = first + width

        def entries(idx, first, count):
            return idx[:, first // LANES : (first + count) // LANES]

        def half_tile(name, h):
            return sb.tile([P, HALF], F32, name=f"{name}{h}")

        x = [half_tile("x", h) for h in range(2)]
        y = [half_tile("y", h) for h in range(2)]
        z = [half_tile("z", h) for h in range(2)]
        work = [half_tile("work", n) for n in range(3)]
        hi = [work[0], work[1]]
        lo = [work[1], work[2]]
        mid = [work[2], work[0]]
        med = sb.tile([P, I], F32, name="med")
        w = sb.tile([P, I], F32, name="w")

        def gather_scalar(dst, idx, h):
            nc.scalar.activation(dst[h][:], a[:].indirect(entries(idx, h * HALF, HALF)), ACT.Copy)

        def gather_vector(dst, idx, h):
            nc.vector.tensor_copy(dst[h][:], a[:].indirect(entries(idx, h * HALF, HALF)))

        def bounds(h):
            nc.vector.tensor_tensor(hi[h][:], x[h][:], y[h][:], ALU.max)
            nc.vector.scalar_tensor_tensor(lo[h][:], x[h][:], top, y[h][:], ALU.min, ALU.min)

        def third(h, first, count):
            part = slice(first, first + count)
            nc.vector.scalar_tensor_tensor(mid[h][:, part], hi[h][:, part], top, z[h][:, part], ALU.min, ALU.min)

        def median(h, first, count):
            part = slice(first, first + count)
            dst = med[:, h * HALF + first : h * HALF + first + count]
            nc.vector.scalar_tensor_tensor(dst, lo[h][:, part], bottom, mid[h][:, part], ALU.max, ALU.max)

        def weight_scalar(h):
            part = slice(h * HALF, (h + 1) * HALF)
            nc.scalar.activation(w[:, part], med[:, part], ACT.Copy, scale=lam_sb[:])

        def put_first(first, count):
            nc.vector.tensor_tensor(
                f1[:].indirect(entries(idx1, first, count)),
                med[:, first : first + count],
                from_lam[:, 0:count],
                ALU.mult,
            )

        def put_second(first, count):
            nc.vector.tensor_copy(f2[:].indirect(entries(idx4, first, count)), w[:, first : first + count])

        blocks = CHUNK // P
        turned = [bank_tile(len(MM_WIDTHS) + c, CHUNK) for c in range(CHUNKS)]

        def add_turned(src, c, opens):
            for b in range(blocks):
                nc.tensor.matmul(
                    turned[c][:, b * P : (b + 1) * P],
                    src[:, T - CHUNK + b * P : T - CHUNK + (b + 1) * P],
                    ident[:],
                    start=(opens and b == 0),
                    stop=(not opens and b == blocks - 1),
                    is_transpose=True,
                )

        for c in range(CHUNKS):
            add_turned(old_sb, c, True)

        gather_vector(x, idx1, 0)
        gather_scalar(y, idx2, 0)
        gather_scalar(z, idx3, 0)
        gather_scalar(x, idx1, 1)
        gather_scalar(y, idx2, 1)
        gather_scalar(z, idx3, 1)
        bounds(0)
        third(0, 0, QUARTER)
        third(0, QUARTER, QUARTER)
        median(0, 0, QUARTER)
        median(0, QUARTER, QUARTER)
        put_first(0, QUARTER)
        bounds(1)
        third(1, 0, HALF)
        put_first(QUARTER, QUARTER)
        median(1, 0, HALF)
        weight_scalar(0)
        weight_scalar(1)
        put_second(0, QUARTER)
        put_first(HALF, HALF)
        put_second(QUARTER, I - QUARTER)

        for c in range(CHUNKS):
            add_turned(f1, c, False)
        base = []
        for c in range(CHUNKS):
            staged = sb.tile([P, CHUNK], F32, name=f"staged{c}")
            nc.scalar.copy(out=staged[:], in_=turned[c][:])
            back = bank_tile(len(MM_WIDTHS) + CHUNKS + c, CHUNK)
            for b in range(blocks):
                nc.tensor.transpose(back[:, b * P : (b + 1) * P], staged[:, b * P : (b + 1) * P], ident[:])
            base.append(back)

        plain_cols = T - CHUNK
        rest = sb.tile([P, plain_cols], F32, name="rest")
        nc.gpsimd.tensor_tensor(rest[:], old_sb[:, 0:plain_cols], f1[:, 0:plain_cols], ALU.add)

        res = sb.tile([P, T], F32, name="res")
        first = 0
        for n, width in enumerate(OUT_WIDTHS):
            cols = slice(first, first + width)
            if first < plain_cols:
                addend = rest[:, cols]
            else:
                addend = base[0][:, first - plain_cols : first - plain_cols + width]
            nc.vector.scalar_tensor_tensor(res[:, cols], f2[:, cols], share_sb[:], addend, ALU.mult, ALU.add)
            queue = nc.sync if n % 2 == 0 else nc.scalar
            queue.dma_start(out=out[:, cols], in_=res[:, cols])
            first = first + width
